import numpy as np
import ml_dtypes


def mxq(x, axis, fmt="e4m3"):
    dtype, down = {"e4m3": (ml_dtypes.float8_e4m3fn, 7), "e5m2": (ml_dtypes.float8_e5m2, 14)}[fmt]
    v = np.moveaxis(np.asarray(x, np.float32).astype(ml_dtypes.bfloat16).astype(np.float64), axis, -1)
    blocks = v.reshape(v.shape[:-1] + (-1, 32))
    amax = np.abs(blocks).max(-1, keepdims=True)
    byte = np.maximum(np.where(amax > 0, np.frexp(amax)[1] - 1 + 127, 0) - down, 1)
    scale = np.exp2(byte - 127.0)
    codes = (blocks / scale).astype(np.float32).astype(dtype).astype(np.float64)
    return np.moveaxis((codes * scale).reshape(v.shape), -1, axis)


WIDE = False


def mx_kscale(k):
    if not WIDE:
        return np.ones(k)
    levels = np.array([10, -10, 5, -5, 0])
    if k % 512:
        return np.exp2(np.random.permutation(np.resize(levels, k // 32))).repeat(32)
    a = np.empty((k // 512, 16))
    for p in range(k // 512):
        a[p, :8] = np.random.permutation(np.resize(levels, 8))
        for g in range(8):
            far = levels[np.abs(levels - a[p, g]) >= 10]
            a[p, g + 8] = far[np.random.randint(len(far))]
    return np.exp2(a.ravel()).repeat(32)


def f64(x):
    return np.asarray(x).astype(np.float64)


def striped(idx):
    return np.tile(idx.reshape(-1, 16).T, (8, 1)).astype(np.uint16)


def unstriped(offs):
    return offs[:16].T.reshape(-1).astype(np.int64)


K, T, E, C, N = 1536, 1024, 6, 256, 256
TOP = 3
PAD = 64


def by_expert(wq, xq):
    return np.concatenate([wq[e].T @ xq[:, e * C:(e + 1) * C] for e in range(E)], axis=1)


def setup_inputs():
    n = np.random.standard_normal
    s = mx_kscale(K)[:, None]
    slot_token = np.empty(E * C, np.int64); pos = np.tile(E * C + np.arange(T) % PAD, (TOP, 1)); taken = np.zeros(T, np.int64)
    liked = np.random.randn(T)
    for e in np.random.permutation(E):
        free = np.flatnonzero(taken < TOP); pick = np.random.permutation(free[np.argsort(-(liked[free] + np.random.gumbel(size=free.size)))[:C]]); slot_token[e * C:(e + 1) * C] = pick
        pos[taken[pick], pick] = e * C + np.arange(C); taken[pick] += 1
    g = np.random.uniform(0.2, 0.8, (TOP, T))
    return {
        "xT": (n((K, T)) * s).astype(np.float32),
        "w": (n((E, K, N)) / np.sqrt(K) / s[None]).astype(np.float32),
        "gate": np.stack([np.tile(r, (N, 1)) for r in g]).astype(np.float32),
        "offs": striped(slot_token),
        "pos1": striped(pos[0]),
        "pos2": striped(pos[1]),
        "pos3": striped(pos[2]),
    }


def reference(xT, w, gate, offs, pos1, pos2, pos3):
    idx = unstriped(offs)
    xq = mxq(f64(xT)[:, idx], 0, "e4m3")
    y = by_expert(mxq(f64(w), 1, "e4m3"), xq)
    y = np.concatenate([y, np.zeros((N, PAD))], axis=1)
    return sum(f64(gate[r]) * y[:, unstriped(p)] for r, p in enumerate((pos1, pos2, pos3)))

@@ -1,0 +1,214 @@
+from contextlib import ExitStack
+
+import concourse.mybir as mybir
+from concourse.masks import make_identity
+
+K, T, E, C, N = 1536, 1024, 6, 256, 256
+TOP, PAD = 3, 64
+SLOTS = E * C
+FLOPS = 2 * K * N * SLOTS
+BYTES = 4 * (K * T + E * K * N + TOP * T + N * T) + 2 * 128 * (SLOTS + TOP * T) // 16
+
+F32 = mybir.dt.float32
+BF16 = mybir.dt.bfloat16
+U32 = mybir.dt.uint32
+I32 = mybir.dt.int32
+U16 = mybir.dt.uint16
+U8 = mybir.dt.uint8
+FP8X4 = mybir.dt.float8_e4m3fn_x4
+COPY = mybir.ActivationFunctionType.Copy
+MULT = mybir.AluOpType.mult
+ADD = mybir.AluOpType.add
+
+P = 128
+PACK = 4
+K_PASS = P * PACK
+PASSES = K // K_PASS
+HALVES = N // P
+X_CHUNK = 512
+GATHER = 512
+SPLIT = 6
+MODE = "CP"
+X_V_COLS = [0,320,0,0,0,0]
+W_V_EVERY = 100
+CHUNKS = [[512,512],[512,256,256]]
+
+
+def cast(engine_copy, dst, src):
+    engine_copy(
+        out=dst.rearrange("p (c i) t -> p c t i", i=4),
+        in_=src.rearrange("p t (c i) -> p c t i", i=4),
+    )
+
+
+def tile_moe_ecr_lin_none_kernel(tc, xT, w, gate, offs, pos1, pos2, pos3, out):
+    nc = tc.nc
+    with ExitStack() as ctx:
+        held = ctx.enter_context(tc.tile_pool(name="held", bufs=1))
+        x_raw = ctx.enter_context(tc.tile_pool(name="x_raw", bufs=1))
+        w_raw = ctx.enter_context(tc.tile_pool(name="w_raw", bufs=1))
+        stage = ctx.enter_context(tc.tile_pool(name="stage", bufs=1))
+        psum = ctx.enter_context(tc.psum_pool(name="psum", bufs=1))
+
+        offs_t = held.tile([P, SLOTS // 16], U16, name="offs_t")
+        pos_t = [held.tile([P, T // 16], U16, name=f"pos_t{r}") for r in range(TOP)]
+        x_words = [held.tile([P, T], U32, name=f"x_words{a}", align_bytes=64) for a in range(PASSES)]
+        x_scales = held.tile([P, T], U8, name="x_scales", align_bytes=64)
+        s_words = [[held.tile([P, GATHER], U32, name=f"s_words{a}_{g}", align_bytes=64) for g in range(SLOTS // GATHER)] for a in range(PASSES)]
+        s_scales = [held.tile([P, GATHER], U8, name=f"s_scales{g}", align_bytes=64) for g in range(SLOTS // GATHER)]
+        y = {}
+        ident = held.tile([P, P], F32, name="ident")
+        gate_cols = held.tile([P, TOP, T // P], F32, name="gate_cols")
+        nc.sync.dma_start(out=gate_cols[:], in_=gate[:, 0, :].rearrange("r (p b) -> p r b", p=P))
+
+        make_identity(nc, ident[:])
+        nc.gpsimd.memset(x_scales[:].bitcast(U32), 0)
+
+        x_tiles = {}
+        for a in range(PASSES):
+            for c in range(T // X_CHUNK):
+                t = x_raw.tile([P, PACK, X_CHUNK], F32, name=f"x_raw{a}_{c}")
+                rows = xT[a * K_PASS : (a + 1) * K_PASS, c * X_CHUNK : (c + 1) * X_CHUNK]
+                nc.sync.dma_start(out=t[:], in_=rows.rearrange("(p j) t -> p j t", j=PACK))
+                x_tiles[a, c] = t
+            if a == 0:
+                nc.sync.dma_start(offs_t[:], offs)
+
+        def gather_words(a, g):
+            cols = slice(g * GATHER // 16, (g + 1) * GATHER // 16)
+            nc.vector.tensor_copy(s_words[a][g][:], x_words[a][:].indirect(offs_t[:, cols]))
+
+        def gather_scales(g):
+            cols = slice(g * GATHER // 16, (g + 1) * GATHER // 16)
+            nc.vector.tensor_copy(s_scales[g][:], x_scales[:].indirect(offs_t[:, cols]))
+
+        for a in range(PASSES):
+            for c in range(T // X_CHUNK):
+                grouped = stage.tile([P, X_CHUNK, PACK], BF16, name="x_grouped", bufs=3, align_bytes=64)
+                v = X_V_COLS[2 * a + c]
+                if v < X_CHUNK:
+                    cast(nc.scalar.copy, grouped[:, v:, :], x_tiles[a, c][:, :, v:])
+                if v > 0:
+                    cast(nc.vector.tensor_copy, grouped[:, :v, :], x_tiles[a, c][:, :, :v])
+                cols = slice(c * X_CHUNK, (c + 1) * X_CHUNK)
+                nc.vector.quantize_mx(out=x_words[a][:, cols].bitcast(FP8X4), scales=x_scales[4 * a :, cols], in_=grouped[:].rearrange("p w j -> p (w j)"))
+            for g in range(SLOTS // GATHER):
+                if a == PASSES - 1:
+                    gather_scales(g)
+                gather_words(a, g)
+
+        gate_full = []
+        for r in range(TOP):
+            full = held.tile([P, P, 2, 4], F32, name=f"gate_full{r}")
+            for c in range(2):
+                spread = psum.tile([P, 4, P], F32, name="spread", tag="turn", bufs=3)
+                for b in range(4):
+                    nc.tensor.transpose(spread[:, b, :], gate_cols[:, r, 4 * c + b : 4 * c + b + 1].to_broadcast([P, P]), ident[:])
+                nc.vector.tensor_copy(out=full[:, :, c, :], in_=spread[:].rearrange("p b q -> p q b"))
+            gate_full.append(full[:].rearrange("p q c b -> p (q c b)"))
+
+        for r, pos in enumerate((pos1, pos2, pos3)):
+            nc.sync.dma_start(pos_t[r][:], pos)
+
+        codes = {}
+        count = [0]
+
+        def load_w(e, a, n0, width, on_vector, hold=None):
+            if hold is None:
+                raw = w_raw.tile([P, PACK, width], F32, name="w_raw", tag=f"w_raw{width}", bufs=(14 if width == P else 6))
+            else:
+                raw = w_raw.tile([P, PACK, width], F32, name="w_raw", tag=hold, bufs=1)
+            rows = w[e, a * K_PASS : (a + 1) * K_PASS, n0 : n0 + width]
+            nc.sync.dma_start(out=raw[:], in_=rows.rearrange("(p j) n -> p j n", j=PACK))
+            grouped = stage.tile([P, width, PACK], BF16, name="w_grouped", tag=f"w_grouped{width}", bufs=(22 if width == P else 6), align_bytes=64)
+            cast(nc.vector.tensor_copy if on_vector else nc.scalar.copy, grouped[:], raw[:])
+            words = held.tile([P, width], U32, name=f"w_words{e}_{a}_{n0}", align_bytes=64)
+            scales = held.tile([P, width], U8, name=f"w_scales{e}_{a}_{n0}", align_bytes=64)
+            nc.vector.quantize_mx(out=words[:].bitcast(FP8X4), scales=scales[:], in_=grouped[:].rearrange("p w j -> p (w j)"))
+            for h in range(n0 // P, (n0 + width) // P):
+                cols = slice(h * P - n0, (h + 1) * P - n0)
+                codes[e, a, h] = (words[:, cols], scales[:, cols])
+
+        def multiply(h):
+            y[h] = w_raw.tile([P, SLOTS + PAD], F32, name="y", tag=f"hold_y{h}", bufs=1)
+            nc.gpsimd.memset(y[h][:, SLOTS:], 0.0)
+            for g in range(SLOTS // GATHER):
+                acc = psum.tile([P, GATHER], F32, name="acc", bufs=3)
+                for e in range(g * GATHER // C, (g + 1) * GATHER // C):
+                    cols = slice(e * C - g * GATHER, (e + 1) * C - g * GATHER)
+                    for a in range(PASSES):
+                        words, scales = codes[e, a, h]
+                        nc.tensor.matmul_mx(out=acc[:, cols], lhsT=words.bitcast(FP8X4), lhsT_scale=scales,
+                                            rhs=s_words[a][g][:, cols].bitcast(FP8X4), rhs_scale=s_scales[g][4 * a :, cols],
+                                            start=(a == 0), stop=(a == PASSES - 1))
+                if g == 2 and h == 1:
+                    nc.vector.tensor_copy(out=y[h][:, g * GATHER : (g + 1) * GATHER], in_=acc[:])
+                else:
+                    nc.scalar.copy(out=y[h][:, g * GATHER : (g + 1) * GATHER], in_=acc[:])
+
+        def combine(h):
+            t0 = 0
+            for width in CHUNKS[h]:
+                cols = slice(t0, t0 + width)
+                lists = slice(t0 // 16, (t0 + width) // 16)
+                blocks = width // P
+                result = stage.tile([P, width], F32, name="result", tag="result", bufs=3)
+                if MODE == "P":
+                    scaled = []
+                    for r in range(TOP):
+                        picked = stage.tile([P, width], F32, name="picked", tag="picked", bufs=6)
+                        nc.vector.tensor_copy(picked[:], y[h][:].indirect(pos_t[r][:, lists]))
+                        turned = psum.tile([P, blocks, P], F32, name="turned", tag="turn", bufs=3)
+                        for b in range(blocks):
+                            nc.tensor.transpose(turned[:, b, :], picked[:, b * P : (b + 1) * P], ident[:])
+                        z = stage.tile([P, blocks, P], F32, name="z", tag="z", bufs=6)
+                        for b in range(blocks):
+                            col = r * 8 + t0 // P + b
+                            nc.scalar.activation(out=z[:, b, :], in_=turned[:, b, :], func=COPY, scale=gate_cols[:, col : col + 1])
+                        scaled.append(z)
+                    back = psum.tile([P, blocks, P], F32, name="back", tag="back", bufs=2)
+                    for b in range(blocks):
+                        for r in range(TOP):
+                            nc.tensor.matmul(back[:, b, :], scaled[r][:, b, :], ident[:], start=(r == 0), stop=(r == TOP - 1), is_transpose=True)
+                    nc.scalar.copy(out=result[:], in_=back[:].rearrange("p b q -> p (b q)"))
+                else:
+                    prods = []
+                    for r in range(TOP):
+                        picked = stage.tile([P, width], F32, name="picked", tag="picked", bufs=6)
+                        nc.vector.tensor_tensor(picked[:], y[h][:].indirect(pos_t[r][:, lists]), gate_full[r][:, cols], MULT)
+                        prods.append(picked)
+                    if MODE == "CV" or (h == 1 and t0 + width == T and True):
+                        part = stage.tile([P, width], F32, name="part", tag="part", bufs=2)
+                        nc.vector.tensor_tensor(part[:], prods[0][:], prods[1][:], ADD)
+                        nc.vector.tensor_tensor(result[:], part[:], prods[2][:], ADD)
+                    else:
+                        summed = psum.tile([P, blocks, P], F32, name="summed", tag="turn", bufs=3)
+                        for b in range(blocks):
+                            for r in range(TOP):
+                                nc.tensor.matmul(summed[:, b, :], prods[r][:, b * P : (b + 1) * P], ident[:], start=(r == 0), stop=(r == TOP - 1), is_transpose=True)
+                        if h == 0:
+                            z = w_raw.tile([P, blocks, P], F32, name="z", tag=f"hold_z{t0}", bufs=1)
+                        else:
+                            z = stage.tile([P, blocks, P], F32, name="z", tag="z", bufs=3)
+                        nc.scalar.copy(out=z[:], in_=summed[:])
+                        back = psum.tile([P, blocks, P], F32, name="back", tag="back", bufs=2)
+                        for b in range(blocks):
+                            nc.tensor.transpose(back[:, b, :], z[:, b, :], ident[:])
+                        nc.scalar.copy(out=result[:], in_=back[:].rearrange("p b q -> p (b q)"))
+                nc.sync.dma_start(out=out[h * P : (h + 1) * P, cols], in_=result[:])
+                t0 += width
+
+        for e in range(E - SPLIT):
+            for a in range(PASSES):
+                load_w(e, a, 0, N, False)
+        units = [(e, a) for e in range(E - SPLIT, E) for a in range(PASSES)]
+        holds = {2: "hold_y0", len(units) - 1: "hold_y1", len(units) - 2: "hold_z0", len(units) - 3: "hold_z512"}
+        for e, a in units:
+            load_w(e, a, 0, P, False)
+        for u, (e, a) in enumerate(units):
+            load_w(e, a, P, P, u % W_V_EVERY == W_V_EVERY - 1, holds.get(u))
+            if u == 2:
+                multiply(0)
+        multiply(1)
+        for h in range(HALVES):
+            combine(h)

@@ -12,11 +12,9 @@ BYTES = 4 * (K * T + E * K * N + TOP * T + N * T) + 2 * 128 * (SLOTS + TOP * T) 
 F32 = mybir.dt.float32
 BF16 = mybir.dt.bfloat16
 U32 = mybir.dt.uint32
-I32 = mybir.dt.int32
 U16 = mybir.dt.uint16
 U8 = mybir.dt.uint8
 FP8X4 = mybir.dt.float8_e4m3fn_x4
-COPY = mybir.ActivationFunctionType.Copy
 MULT = mybir.AluOpType.mult
 ADD = mybir.AluOpType.add
 
@@ -25,13 +23,16 @@ PACK = 4
 K_PASS = P * PACK
 PASSES = K // K_PASS
 HALVES = N // P
+BANK = 512
 X_CHUNK = 512
-GATHER = 512
-SPLIT = 6
-MODE = "CP"
-X_V_COLS = [0,320,0,0,0,0]
-W_V_EVERY = 100
-CHUNKS = [[512,512],[512,256,256]]
+GATHER = 768
+SPLIT = 3
+X_V_COLS = [0,0,0,0,0,0]
+V_UNITS = [3,5,7]
+V_FULL = []
+CHUNKS = [[1024],[512,256,256]]
+V_PAIRS = {1: 7, 3: 8}
+GATE_EARLY = 3
 
 
 def cast(engine_copy, dst, src):
@@ -45,60 +46,38 @@ def tile_moe_ecr_lin_none_kernel(tc, xT, w, gate, offs, pos1, pos2, pos3, out):
     nc = tc.nc
     with ExitStack() as ctx:
         held = ctx.enter_context(tc.tile_pool(name="held", bufs=1))
-        x_raw = ctx.enter_context(tc.tile_pool(name="x_raw", bufs=1))
-        w_raw = ctx.enter_context(tc.tile_pool(name="w_raw", bufs=1))
+        raws = ctx.enter_context(tc.tile_pool(name="raws", bufs=1))
         stage = ctx.enter_context(tc.tile_pool(name="stage", bufs=1))
         psum = ctx.enter_context(tc.psum_pool(name="psum", bufs=1))
 
         offs_t = held.tile([P, SLOTS // 16], U16, name="offs_t")
         pos_t = [held.tile([P, T // 16], U16, name=f"pos_t{r}") for r in range(TOP)]
-        x_words = [held.tile([P, T], U32, name=f"x_words{a}", align_bytes=64) for a in range(PASSES)]
         x_scales = held.tile([P, T], U8, name="x_scales", align_bytes=64)
         s_words = [[held.tile([P, GATHER], U32, name=f"s_words{a}_{g}", align_bytes=64) for g in range(SLOTS // GATHER)] for a in range(PASSES)]
         s_scales = [held.tile([P, GATHER], U8, name=f"s_scales{g}", align_bytes=64) for g in range(SLOTS // GATHER)]
-        y = {}
         ident = held.tile([P, P], F32, name="ident")
-        gate_cols = held.tile([P, TOP, T // P], F32, name="gate_cols")
-        nc.sync.dma_start(out=gate_cols[:], in_=gate[:, 0, :].rearrange("r (p b) -> p r b", p=P))
+        gate_cols = held.tile([P, TOP, T // P], F32, name="gate_cols", tag="hold_gate", align_bytes=64)
+        y = {}
 
+        nc.sync.dma_start(out=gate_cols[:], in_=gate[:, 0, :].rearrange("r (p b) -> p r b", p=P))
         make_identity(nc, ident[:])
         nc.gpsimd.memset(x_scales[:].bitcast(U32), 0)
+        y[0] = held.tile([P, SLOTS + PAD], F32, name="y0")
+        nc.gpsimd.memset(y[0][:, SLOTS:], 0.0)
 
         x_tiles = {}
         for a in range(PASSES):
             for c in range(T // X_CHUNK):
-                t = x_raw.tile([P, PACK, X_CHUNK], F32, name=f"x_raw{a}_{c}")
+                t = raws.tile([P, PACK, X_CHUNK], F32, name="x_raw", bufs=6)
                 rows = xT[a * K_PASS : (a + 1) * K_PASS, c * X_CHUNK : (c + 1) * X_CHUNK]
                 nc.sync.dma_start(out=t[:], in_=rows.rearrange("(p j) t -> p j t", j=PACK))
                 x_tiles[a, c] = t
             if a == 0:
                 nc.sync.dma_start(offs_t[:], offs)
 
-        def gather_words(a, g):
-            cols = slice(g * GATHER // 16, (g + 1) * GATHER // 16)
-            nc.vector.tensor_copy(s_words[a][g][:], x_words[a][:].indirect(offs_t[:, cols]))
-
-        def gather_scales(g):
-            cols = slice(g * GATHER // 16, (g + 1) * GATHER // 16)
-            nc.vector.tensor_copy(s_scales[g][:], x_scales[:].indirect(offs_t[:, cols]))
-
-        for a in range(PASSES):
-            for c in range(T // X_CHUNK):
-                grouped = stage.tile([P, X_CHUNK, PACK], BF16, name="x_grouped", bufs=3, align_bytes=64)
-                v = X_V_COLS[2 * a + c]
-                if v < X_CHUNK:
-                    cast(nc.scalar.copy, grouped[:, v:, :], x_tiles[a, c][:, :, v:])
-                if v > 0:
-                    cast(nc.vector.tensor_copy, grouped[:, :v, :], x_tiles[a, c][:, :, :v])
-                cols = slice(c * X_CHUNK, (c + 1) * X_CHUNK)
-                nc.vector.quantize_mx(out=x_words[a][:, cols].bitcast(FP8X4), scales=x_scales[4 * a :, cols], in_=grouped[:].rearrange("p w j -> p (w j)"))
-            for g in range(SLOTS // GATHER):
-                if a == PASSES - 1:
-                    gather_scales(g)
-                gather_words(a, g)
-
         gate_full = []
-        for r in range(TOP):
+
+        def spread_gate(r):
             full = held.tile([P, P, 2, 4], F32, name=f"gate_full{r}")
             for c in range(2):
                 spread = psum.tile([P, 4, P], F32, name="spread", tag="turn", bufs=3)
@@ -107,108 +86,139 @@ def tile_moe_ecr_lin_none_kernel(tc, xT, w, gate, offs, pos1, pos2, pos3, out):
                 nc.vector.tensor_copy(out=full[:, :, c, :], in_=spread[:].rearrange("p b q -> p q b"))
             gate_full.append(full[:].rearrange("p q c b -> p (q c b)"))
 
+        for r in range(GATE_EARLY):
+            spread_gate(r)
+
+        x_words = {}
+        for a in range(PASSES):
+            x_words[a] = held.tile([P, T], U32, name="x_words", tag="hold_gate", align_bytes=64)
+            for c in range(T // X_CHUNK):
+                grouped = stage.tile([P, X_CHUNK, PACK], BF16, name="x_grouped", tag="wide", bufs=7, align_bytes=64)
+                v = X_V_COLS[2 * a + c]
+                if v < X_CHUNK:
+                    cast(nc.scalar.copy, grouped[:, v:, :], x_tiles[a, c][:, :, v:])
+                if v > 0:
+                    cast(nc.vector.tensor_copy, grouped[:, :v, :], x_tiles[a, c][:, :, :v])
+                cols = slice(c * X_CHUNK, (c + 1) * X_CHUNK)
+                nc.vector.quantize_mx(out=x_words[a][:, cols].bitcast(FP8X4), scales=x_scales[4 * a :, cols], in_=grouped[:].rearrange("p w j -> p (w j)"))
+            for g in range(SLOTS // GATHER):
+                lists = offs_t[:, g * GATHER // 16 : (g + 1) * GATHER // 16]
+                if a == PASSES - 1:
+                    nc.vector.tensor_copy(s_scales[g][:], x_scales[:].indirect(lists))
+                nc.vector.tensor_copy(s_words[a][g][:], x_words[a][:].indirect(lists))
+
+        for r in range(GATE_EARLY, TOP):
+            spread_gate(r)
+
         for r, pos in enumerate((pos1, pos2, pos3)):
             nc.sync.dma_start(pos_t[r][:], pos)
 
         codes = {}
-        count = [0]
 
-        def load_w(e, a, n0, width, on_vector, hold=None):
-            if hold is None:
-                raw = w_raw.tile([P, PACK, width], F32, name="w_raw", tag=f"w_raw{width}", bufs=(14 if width == P else 6))
+        def quantize_w(units, raw_tags, grouped_tag, on_vector):
+            total = sum(u[3] for u in units)
+            if grouped_tag is None:
+                grouped = stage.tile([P, total, PACK], BF16, name="w_grouped", bufs=10, align_bytes=64)
             else:
-                raw = w_raw.tile([P, PACK, width], F32, name="w_raw", tag=hold, bufs=1)
-            rows = w[e, a * K_PASS : (a + 1) * K_PASS, n0 : n0 + width]
-            nc.sync.dma_start(out=raw[:], in_=rows.rearrange("(p j) n -> p j n", j=PACK))
-            grouped = stage.tile([P, width, PACK], BF16, name="w_grouped", tag=f"w_grouped{width}", bufs=(22 if width == P else 6), align_bytes=64)
-            cast(nc.vector.tensor_copy if on_vector else nc.scalar.copy, grouped[:], raw[:])
-            words = held.tile([P, width], U32, name=f"w_words{e}_{a}_{n0}", align_bytes=64)
-            scales = held.tile([P, width], U8, name=f"w_scales{e}_{a}_{n0}", align_bytes=64)
+                grouped = stage.tile([P, total, PACK], BF16, name="w_grouped_held", tag=grouped_tag, bufs=1, align_bytes=64)
+            c0 = 0
+            for (e, a, n0, width), tag, v in zip(units, raw_tags, on_vector):
+                if tag is None:
+                    raw = raws.tile([P, PACK, width], F32, name="w_raw", bufs=9)
+                else:
+                    raw = raws.tile([P, PACK, width], F32, name="w_raw_held", tag=tag, bufs=1)
+                rows = w[e, a * K_PASS : (a + 1) * K_PASS, n0 : n0 + width]
+                nc.sync.dma_start(out=raw[:], in_=rows.rearrange("(p j) n -> p j n", j=PACK))
+                cast(nc.vector.tensor_copy if v else nc.scalar.copy, grouped[:, c0 : c0 + width, :], raw[:])
+                c0 += width
+            e, a, n0, width = units[0]
+            words = held.tile([P, total], U32, name=f"w_words{e}_{a}_{n0}", align_bytes=64)
+            scales = held.tile([P, total], U8, name=f"w_scales{e}_{a}_{n0}", align_bytes=64)
             nc.vector.quantize_mx(out=words[:].bitcast(FP8X4), scales=scales[:], in_=grouped[:].rearrange("p w j -> p (w j)"))
-            for h in range(n0 // P, (n0 + width) // P):
-                cols = slice(h * P - n0, (h + 1) * P - n0)
-                codes[e, a, h] = (words[:, cols], scales[:, cols])
+            c0 = 0
+            for e, a, n0, width in units:
+                for h in range(n0 // P, (n0 + width) // P):
+                    codes[e, a, h] = (words[:, c0 : c0 + P], scales[:, c0 : c0 + P])
+                    c0 += P
 
         def multiply(h):
-            y[h] = w_raw.tile([P, SLOTS + PAD], F32, name="y", tag=f"hold_y{h}", bufs=1)
-            nc.gpsimd.memset(y[h][:, SLOTS:], 0.0)
-            for g in range(SLOTS // GATHER):
-                acc = psum.tile([P, GATHER], F32, name="acc", bufs=3)
-                for e in range(g * GATHER // C, (g + 1) * GATHER // C):
-                    cols = slice(e * C - g * GATHER, (e + 1) * C - g * GATHER)
+            for b in range(SLOTS // BANK):
+                acc = psum.tile([P, BANK], F32, name="acc", bufs=3)
+                for e in range(b * BANK // C, (b + 1) * BANK // C):
+                    g, c0 = divmod(e * C, GATHER)
+                    cols = slice(c0, c0 + C)
                     for a in range(PASSES):
                         words, scales = codes[e, a, h]
-                        nc.tensor.matmul_mx(out=acc[:, cols], lhsT=words.bitcast(FP8X4), lhsT_scale=scales,
+                        nc.tensor.matmul_mx(out=acc[:, e * C - b * BANK : (e + 1) * C - b * BANK], lhsT=words.bitcast(FP8X4), lhsT_scale=scales,
                                             rhs=s_words[a][g][:, cols].bitcast(FP8X4), rhs_scale=s_scales[g][4 * a :, cols],
                                             start=(a == 0), stop=(a == PASSES - 1))
-                if g == 2 and h == 1:
-                    nc.vector.tensor_copy(out=y[h][:, g * GATHER : (g + 1) * GATHER], in_=acc[:])
+                if h == 0:
+                    nc.vector.tensor_copy(out=y[h][:, b * BANK : (b + 1) * BANK], in_=acc[:])
                 else:
-                    nc.scalar.copy(out=y[h][:, g * GATHER : (g + 1) * GATHER], in_=acc[:])
+                    nc.scalar.copy(out=y[h][:, b * BANK : (b + 1) * BANK], in_=acc[:])
 
-        def combine(h):
+        def combine(h, holds):
             t0 = 0
             for width in CHUNKS[h]:
-                cols = slice(t0, t0 + width)
                 lists = slice(t0 // 16, (t0 + width) // 16)
-                blocks = width // P
-                result = stage.tile([P, width], F32, name="result", tag="result", bufs=3)
-                if MODE == "P":
-                    scaled = []
-                    for r in range(TOP):
-                        picked = stage.tile([P, width], F32, name="picked", tag="picked", bufs=6)
-                        nc.vector.tensor_copy(picked[:], y[h][:].indirect(pos_t[r][:, lists]))
-                        turned = psum.tile([P, blocks, P], F32, name="turned", tag="turn", bufs=3)
-                        for b in range(blocks):
-                            nc.tensor.transpose(turned[:, b, :], picked[:, b * P : (b + 1) * P], ident[:])
-                        z = stage.tile([P, blocks, P], F32, name="z", tag="z", bufs=6)
-                        for b in range(blocks):
-                            col = r * 8 + t0 // P + b
-                            nc.scalar.activation(out=z[:, b, :], in_=turned[:, b, :], func=COPY, scale=gate_cols[:, col : col + 1])
-                        scaled.append(z)
-                    back = psum.tile([P, blocks, P], F32, name="back", tag="back", bufs=2)
-                    for b in range(blocks):
-                        for r in range(TOP):
-                            nc.tensor.matmul(back[:, b, :], scaled[r][:, b, :], ident[:], start=(r == 0), stop=(r == TOP - 1), is_transpose=True)
-                    nc.scalar.copy(out=result[:], in_=back[:].rearrange("p b q -> p (b q)"))
-                else:
-                    prods = []
-                    for r in range(TOP):
-                        picked = stage.tile([P, width], F32, name="picked", tag="picked", bufs=6)
-                        nc.vector.tensor_tensor(picked[:], y[h][:].indirect(pos_t[r][:, lists]), gate_full[r][:, cols], MULT)
-                        prods.append(picked)
-                    if MODE == "CV" or (h == 1 and t0 + width == T and True):
-                        part = stage.tile([P, width], F32, name="part", tag="part", bufs=2)
-                        nc.vector.tensor_tensor(part[:], prods[0][:], prods[1][:], ADD)
-                        nc.vector.tensor_tensor(result[:], part[:], prods[2][:], ADD)
+                prods = []
+                for r in range(TOP):
+                    if r in holds:
+                        picked = stage.tile([P, width], F32, name="picked_held", tag=holds[r], bufs=1, align_bytes=64)
                     else:
+                        picked = stage.tile([P, width], F32, name="picked", tag="wide", bufs=7, align_bytes=64)
+                    nc.vector.tensor_tensor(picked[:], y[h][:].indirect(pos_t[r][:, lists]), gate_full[r][:, t0 : t0 + width], MULT)
+                    prods.append(picked)
+                if h == HALVES - 1 and t0 + width == T:
+                    part = stage.tile([P, width], F32, name="part")
+                    result = stage.tile([P, width], F32, name="result", bufs=3)
+                    nc.vector.tensor_tensor(part[:], prods[0][:], prods[1][:], ADD)
+                    nc.vector.tensor_tensor(result[:], part[:], prods[2][:], ADD)
+                    nc.sync.dma_start(out=out[h * P : (h + 1) * P, t0 : t0 + width], in_=result[:])
+                else:
+                    for s0 in range(0, width, BANK):
+                        span = min(BANK, width - s0)
+                        blocks = span // P
                         summed = psum.tile([P, blocks, P], F32, name="summed", tag="turn", bufs=3)
                         for b in range(blocks):
                             for r in range(TOP):
-                                nc.tensor.matmul(summed[:, b, :], prods[r][:, b * P : (b + 1) * P], ident[:], start=(r == 0), stop=(r == TOP - 1), is_transpose=True)
-                        if h == 0:
-                            z = w_raw.tile([P, blocks, P], F32, name="z", tag=f"hold_z{t0}", bufs=1)
-                        else:
-                            z = stage.tile([P, blocks, P], F32, name="z", tag="z", bufs=3)
+                                nc.tensor.matmul(summed[:, b, :], prods[r][:, s0 + b * P : s0 + (b + 1) * P], ident[:], start=(r == 0), stop=(r == TOP - 1), is_transpose=True)
+                        z = stage.tile([P, blocks, P], F32, name="z", bufs=2)
                         nc.scalar.copy(out=z[:], in_=summed[:])
-                        back = psum.tile([P, blocks, P], F32, name="back", tag="back", bufs=2)
+                        back = psum.tile([P, blocks, P], F32, name="back", bufs=2)
                         for b in range(blocks):
                             nc.tensor.transpose(back[:, b, :], z[:, b, :], ident[:])
+                        result = stage.tile([P, span], F32, name="result", bufs=3)
                         nc.scalar.copy(out=result[:], in_=back[:].rearrange("p b q -> p (b q)"))
-                nc.sync.dma_start(out=out[h * P : (h + 1) * P, cols], in_=result[:])
+                        nc.sync.dma_start(out=out[h * P : (h + 1) * P, t0 + s0 : t0 + s0 + span], in_=result[:])
                 t0 += width
 
+        u = 0
         for e in range(E - SPLIT):
             for a in range(PASSES):
-                load_w(e, a, 0, N, False)
-        units = [(e, a) for e in range(E - SPLIT, E) for a in range(PASSES)]
-        holds = {2: "hold_y0", len(units) - 1: "hold_y1", len(units) - 2: "hold_z0", len(units) - 3: "hold_z512"}
-        for e, a in units:
-            load_w(e, a, 0, P, False)
-        for u, (e, a) in enumerate(units):
-            load_w(e, a, P, P, u % W_V_EVERY == W_V_EVERY - 1, holds.get(u))
-            if u == 2:
-                multiply(0)
-        multiply(1)
+                quantize_w([(e, a, 0, N)], [None], (f"hold_v{u}" if u in V_PAIRS.values() else None), [False])
+                u += 1
         for h in range(HALVES):
-            combine(h)
+            units = [(e, a, h * P, P) for e in range(E - SPLIT, E) for a in range(PASSES)]
+            starts = list(range(0, len(units), 2))
+            for s in starts:
+                group = units[s : s + 2]
+                last = h == 1 and s == starts[-1]
+                raw_tags = [None] * len(group)
+                grouped_tag = None
+                if s == starts[-1]:
+                    raw_tags[-1] = "hold_y1"
+                if last:
+                    grouped_tag = "hold_p2"
+                elif h == 1 and s == starts[1]:
+                    grouped_tag = "hold_p1"
+                on_v = h == 0 and s // 2 in V_PAIRS
+                if on_v:
+                    grouped_tag = f"hold_v{V_PAIRS[s // 2]}"
+                quantize_w(group, raw_tags, grouped_tag, [on_v] * len(group))
+            if h == 1:
+                y[1] = raws.tile([P, SLOTS + PAD], F32, name="y1", tag="hold_y1", bufs=1)
+                nc.gpsimd.memset(y[1][:, SLOTS:], 0.0)
+            multiply(h)
+        combine(0, {1: "hold_p1", 2: "hold_p2"})
+        combine(1, {})

@@ -26,12 +26,13 @@ HALVES = N // P
 BANK = 512
 X_CHUNK = 512
 GATHER = 768
-SPLIT = 3
+SPLIT = 2
 X_V_COLS = [0,0,0,0,0,0]
 V_UNITS = [3,5,7]
 V_FULL = []
 CHUNKS = [[1024],[512,256,256]]
-V_PAIRS = {1: 7, 3: 8}
+V_PAIRS = {2: 8}
+V_GROUPS = {10: 6, 13: 11}
 GATE_EARLY = 3
 
 
@@ -62,8 +63,6 @@ def tile_moe_ecr_lin_none_kernel(tc, xT, w, gate, offs, pos1, pos2, pos3, out):
         nc.sync.dma_start(out=gate_cols[:], in_=gate[:, 0, :].rearrange("r (p b) -> p r b", p=P))
         make_identity(nc, ident[:])
         nc.gpsimd.memset(x_scales[:].bitcast(U32), 0)
-        y[0] = held.tile([P, SLOTS + PAD], F32, name="y0")
-        nc.gpsimd.memset(y[0][:, SLOTS:], 0.0)
 
         x_tiles = {}
         for a in range(PASSES):
@@ -118,13 +117,13 @@ def tile_moe_ecr_lin_none_kernel(tc, xT, w, gate, offs, pos1, pos2, pos3, out):
         def quantize_w(units, raw_tags, grouped_tag, on_vector):
             total = sum(u[3] for u in units)
             if grouped_tag is None:
-                grouped = stage.tile([P, total, PACK], BF16, name="w_grouped", bufs=10, align_bytes=64)
+                grouped = stage.tile([P, total, PACK], BF16, name="w_grouped", bufs=11, align_bytes=64)
             else:
                 grouped = stage.tile([P, total, PACK], BF16, name="w_grouped_held", tag=grouped_tag, bufs=1, align_bytes=64)
             c0 = 0
             for (e, a, n0, width), tag, v in zip(units, raw_tags, on_vector):
                 if tag is None:
-                    raw = raws.tile([P, PACK, width], F32, name="w_raw", bufs=9)
+                    raw = raws.tile([P, PACK, width], F32, name="w_raw", bufs=8)
                 else:
                     raw = raws.tile([P, PACK, width], F32, name="w_raw_held", tag=tag, bufs=1)
                 rows = w[e, a * K_PASS : (a + 1) * K_PASS, n0 : n0 + width]
@@ -152,10 +151,7 @@ def tile_moe_ecr_lin_none_kernel(tc, xT, w, gate, offs, pos1, pos2, pos3, out):
                         nc.tensor.matmul_mx(out=acc[:, e * C - b * BANK : (e + 1) * C - b * BANK], lhsT=words.bitcast(FP8X4), lhsT_scale=scales,
                                             rhs=s_words[a][g][:, cols].bitcast(FP8X4), rhs_scale=s_scales[g][4 * a :, cols],
                                             start=(a == 0), stop=(a == PASSES - 1))
-                if h == 0:
-                    nc.vector.tensor_copy(out=y[h][:, b * BANK : (b + 1) * BANK], in_=acc[:])
-                else:
-                    nc.scalar.copy(out=y[h][:, b * BANK : (b + 1) * BANK], in_=acc[:])
+                nc.scalar.copy(out=y[h][:, b * BANK : (b + 1) * BANK], in_=acc[:])
 
         def combine(h, holds):
             t0 = 0
@@ -193,32 +189,23 @@ def tile_moe_ecr_lin_none_kernel(tc, xT, w, gate, offs, pos1, pos2, pos3, out):
                         nc.sync.dma_start(out=out[h * P : (h + 1) * P, t0 + s0 : t0 + s0 + span], in_=result[:])
                 t0 += width
 
-        u = 0
-        for e in range(E - SPLIT):
-            for a in range(PASSES):
-                quantize_w([(e, a, 0, N)], [None], (f"hold_v{u}" if u in V_PAIRS.values() else None), [False])
-                u += 1
+        groups = [[(e, a, 0, N)] for e in range(E - SPLIT) for a in range(PASSES)]
+        ends = []
         for h in range(HALVES):
             units = [(e, a, h * P, P) for e in range(E - SPLIT, E) for a in range(PASSES)]
-            starts = list(range(0, len(units), 2))
-            for s in starts:
-                group = units[s : s + 2]
-                last = h == 1 and s == starts[-1]
-                raw_tags = [None] * len(group)
-                grouped_tag = None
-                if s == starts[-1]:
-                    raw_tags[-1] = "hold_y1"
-                if last:
-                    grouped_tag = "hold_p2"
-                elif h == 1 and s == starts[1]:
-                    grouped_tag = "hold_p1"
-                on_v = h == 0 and s // 2 in V_PAIRS
-                if on_v:
-                    grouped_tag = f"hold_v{V_PAIRS[s // 2]}"
-                quantize_w(group, raw_tags, grouped_tag, [on_v] * len(group))
-            if h == 1:
-                y[1] = raws.tile([P, SLOTS + PAD], F32, name="y1", tag="hold_y1", bufs=1)
-                nc.gpsimd.memset(y[1][:, SLOTS:], 0.0)
-            multiply(h)
+            groups.extend(units[s : s + 2] for s in range(0, len(units), 2))
+            ends.append(len(groups) - 1)
+        grouped_tags = {ends[1]: "hold_p2", ends[0] + 1: "hold_p1"}
+        for late, early in V_GROUPS.items():
+            grouped_tags[late] = f"hold_v{late}"
+            grouped_tags[early] = f"hold_v{late}"
+        raw_tags = {ends[0]: "hold_y0", ends[1]: "hold_y1", 7: "hold_y0", 11: "hold_y1"}
+        for i, group in enumerate(groups):
+            quantize_w(group, [None] * (len(group) - 1) + [raw_tags.get(i)], grouped_tags.get(i), [i in V_GROUPS] * len(group))
+            if i in ends:
+                h = ends.index(i)
+                y[h] = raws.tile([P, SLOTS + PAD], F32, name="y", tag=f"hold_y{h}", bufs=1)
+                nc.gpsimd.memset(y[h][:, SLOTS:], 0.0)
+                multiply(h)
         combine(0, {1: "hold_p1", 2: "hold_p2"})
         combine(1, {})

@@ -32,7 +32,8 @@ V_UNITS = [3,5,7]
 V_FULL = []
 CHUNKS = [[1024],[512,256,256]]
 V_PAIRS = {2: 8}
-V_GROUPS = {10: 6, 13: 11}
+V_GROUPS = {10: 7, 12: 9, 13: 11}
+X_SHARE = 256
 GATE_EARLY = 3
 
 
@@ -57,7 +58,7 @@ def tile_moe_ecr_lin_none_kernel(tc, xT, w, gate, offs, pos1, pos2, pos3, out):
         s_words = [[held.tile([P, GATHER], U32, name=f"s_words{a}_{g}", align_bytes=64) for g in range(SLOTS // GATHER)] for a in range(PASSES)]
         s_scales = [held.tile([P, GATHER], U8, name=f"s_scales{g}", align_bytes=64) for g in range(SLOTS // GATHER)]
         ident = held.tile([P, P], F32, name="ident")
-        gate_cols = held.tile([P, TOP, T // P], F32, name="gate_cols", tag="hold_gate", align_bytes=64)
+        gate_cols = raws.tile([P, TOP, T // P], F32, name="gate_cols", tag="hold_gate", align_bytes=64)
         y = {}
 
         nc.sync.dma_start(out=gate_cols[:], in_=gate[:, 0, :].rearrange("r (p b) -> p r b", p=P))
@@ -67,7 +68,7 @@ def tile_moe_ecr_lin_none_kernel(tc, xT, w, gate, offs, pos1, pos2, pos3, out):
         x_tiles = {}
         for a in range(PASSES):
             for c in range(T // X_CHUNK):
-                t = raws.tile([P, PACK, X_CHUNK], F32, name="x_raw", bufs=6)
+                t = raws.tile([P, PACK, X_CHUNK], F32, name="x_raw", tag=f"x_raw{a}_{c}", align_bytes=64)
                 rows = xT[a * K_PASS : (a + 1) * K_PASS, c * X_CHUNK : (c + 1) * X_CHUNK]
                 nc.sync.dma_start(out=t[:], in_=rows.rearrange("(p j) t -> p j t", j=PACK))
                 x_tiles[a, c] = t
@@ -90,16 +91,19 @@ def tile_moe_ecr_lin_none_kernel(tc, xT, w, gate, offs, pos1, pos2, pos3, out):
 
         x_words = {}
         for a in range(PASSES):
-            x_words[a] = held.tile([P, T], U32, name="x_words", tag="hold_gate", align_bytes=64)
-            for c in range(T // X_CHUNK):
-                grouped = stage.tile([P, X_CHUNK, PACK], BF16, name="x_grouped", tag="wide", bufs=7, align_bytes=64)
-                v = X_V_COLS[2 * a + c]
-                if v < X_CHUNK:
-                    cast(nc.scalar.copy, grouped[:, v:, :], x_tiles[a, c][:, :, v:])
-                if v > 0:
-                    cast(nc.vector.tensor_copy, grouped[:, :v, :], x_tiles[a, c][:, :, :v])
-                cols = slice(c * X_CHUNK, (c + 1) * X_CHUNK)
+            split = X_CHUNK - X_SHARE
+            first = stage.tile([P, X_CHUNK, PACK], BF16, name="x_grouped", tag="wide", bufs=7, align_bytes=64)
+            cast(nc.scalar.copy, first[:], x_tiles[a, 0][:])
+            second = stage.tile([P, split, PACK], BF16, name="x_grouped", tag="wide", bufs=7, align_bytes=64)
+            cast(nc.scalar.copy, second[:], x_tiles[a, 1][:, :, :split])
+            third = raws.tile([P, X_SHARE, PACK], BF16, name="x_share", tag=("hold_gate" if a == 0 else f"x_raw{a - 1}_1"), align_bytes=64)
+            cast(nc.vector.tensor_copy, third[:], x_tiles[a, 1][:, :, split:])
+            x_words[a] = raws.tile([P, T], U32, name="x_words", tag=f"x_raw{a}_1", align_bytes=64)
+            t0 = 0
+            for grouped in (first, second, third):
+                cols = slice(t0, t0 + grouped.shape[1])
                 nc.vector.quantize_mx(out=x_words[a][:, cols].bitcast(FP8X4), scales=x_scales[4 * a :, cols], in_=grouped[:].rearrange("p w j -> p (w j)"))
+                t0 += grouped.shape[1]
             for g in range(SLOTS // GATHER):
                 lists = offs_t[:, g * GATHER // 16 : (g + 1) * GATHER // 16]
                 if a == PASSES - 1:
@@ -117,7 +121,7 @@ def tile_moe_ecr_lin_none_kernel(tc, xT, w, gate, offs, pos1, pos2, pos3, out):
         def quantize_w(units, raw_tags, grouped_tag, on_vector):
             total = sum(u[3] for u in units)
             if grouped_tag is None:
-                grouped = stage.tile([P, total, PACK], BF16, name="w_grouped", bufs=11, align_bytes=64)
+                grouped = stage.tile([P, total, PACK], BF16, name="w_grouped", bufs=9, align_bytes=64)
             else:
                 grouped = stage.tile([P, total, PACK], BF16, name="w_grouped_held", tag=grouped_tag, bufs=1, align_bytes=64)
             c0 = 0

from contextlib import ExitStack

import concourse.mybir as mybir
from concourse.masks import make_identity

K, T, E, C, N = 1536, 1024, 6, 256, 256
TOP, PAD = 3, 64
SLOTS = E * C
FLOPS = 2 * K * N * SLOTS
BYTES = 4 * (K * T + E * K * N + TOP * T + N * T) + 2 * 128 * (SLOTS + TOP * T) // 16

F32 = mybir.dt.float32
BF16 = mybir.dt.bfloat16
U32 = mybir.dt.uint32
U16 = mybir.dt.uint16
U8 = mybir.dt.uint8
FP8X4 = mybir.dt.float8_e4m3fn_x4
MULT = mybir.AluOpType.mult
ADD = mybir.AluOpType.add

P = 128
PACK = 4
K_PASS = P * PACK
PASSES = K // K_PASS
HALVES = N // P
BANK = 512
X_CHUNK = 512
GATHER = 768
SPLIT = 2
X_V_COLS = [0,0,0,0,0,0]
V_UNITS = [3,5,7]
V_FULL = []
CHUNKS = [[1024],[512,256,256]]
V_PAIRS = {2: 8}
V_GROUPS = {10: 7, 12: 9, 13: 11}
X_SHARE = 256
GATE_EARLY = 3


def cast(engine_copy, dst, src):
    engine_copy(
        out=dst.rearrange("p (c i) t -> p c t i", i=4),
        in_=src.rearrange("p t (c i) -> p c t i", i=4),
    )


def tile_moe_ecr_lin_none_kernel(tc, xT, w, gate, offs, pos1, pos2, pos3, out):
    nc = tc.nc
    with ExitStack() as ctx:
        held = ctx.enter_context(tc.tile_pool(name="held", bufs=1))
        raws = ctx.enter_context(tc.tile_pool(name="raws", bufs=1))
        stage = ctx.enter_context(tc.tile_pool(name="stage", bufs=1))
        psum = ctx.enter_context(tc.psum_pool(name="psum", bufs=1))

        offs_t = held.tile([P, SLOTS // 16], U16, name="offs_t")
        pos_t = [held.tile([P, T // 16], U16, name=f"pos_t{r}") for r in range(TOP)]
        x_scales = held.tile([P, T], U8, name="x_scales", align_bytes=64)
        s_words = [[held.tile([P, GATHER], U32, name=f"s_words{a}_{g}", align_bytes=64) for g in range(SLOTS // GATHER)] for a in range(PASSES)]
        s_scales = [held.tile([P, GATHER], U8, name=f"s_scales{g}", align_bytes=64) for g in range(SLOTS // GATHER)]
        ident = held.tile([P, P], F32, name="ident")
        gate_cols = raws.tile([P, TOP, T // P], F32, name="gate_cols", tag="hold_gate", align_bytes=64)
        y = {}

        nc.sync.dma_start(out=gate_cols[:], in_=gate[:, 0, :].rearrange("r (p b) -> p r b", p=P))
        make_identity(nc, ident[:])
        nc.gpsimd.memset(x_scales[:].bitcast(U32), 0)

        x_tiles = {}
        for a in range(PASSES):
            for c in range(T // X_CHUNK):
                t = raws.tile([P, PACK, X_CHUNK], F32, name="x_raw", tag=f"x_raw{a}_{c}", align_bytes=64)
                rows = xT[a * K_PASS : (a + 1) * K_PASS, c * X_CHUNK : (c + 1) * X_CHUNK]
                nc.sync.dma_start(out=t[:], in_=rows.rearrange("(p j) t -> p j t", j=PACK))
                x_tiles[a, c] = t
            if a == 0:
                nc.sync.dma_start(offs_t[:], offs)

        gate_full = []

        def spread_gate(r):
            full = held.tile([P, P, 2, 4], F32, name=f"gate_full{r}")
            for c in range(2):
                spread = psum.tile([P, 4, P], F32, name="spread", tag="turn", bufs=3)
                for b in range(4):
                    nc.tensor.transpose(spread[:, b, :], gate_cols[:, r, 4 * c + b : 4 * c + b + 1].to_broadcast([P, P]), ident[:])
                nc.vector.tensor_copy(out=full[:, :, c, :], in_=spread[:].rearrange("p b q -> p q b"))
            gate_full.append(full[:].rearrange("p q c b -> p (q c b)"))

        for r in range(GATE_EARLY):
            spread_gate(r)

        x_words = {}
        for a in range(PASSES):
            split = X_CHUNK - X_SHARE
            first = stage.tile([P, X_CHUNK, PACK], BF16, name="x_grouped", tag="wide", bufs=7, align_bytes=64)
            cast(nc.scalar.copy, first[:], x_tiles[a, 0][:])
            second = stage.tile([P, split, PACK], BF16, name="x_grouped", tag="wide", bufs=7, align_bytes=64)
            cast(nc.scalar.copy, second[:], x_tiles[a, 1][:, :, :split])
            third = raws.tile([P, X_SHARE, PACK], BF16, name="x_share", tag=("hold_gate" if a == 0 else f"x_raw{a - 1}_1"), align_bytes=64)
            cast(nc.vector.tensor_copy, third[:], x_tiles[a, 1][:, :, split:])
            x_words[a] = raws.tile([P, T], U32, name="x_words", tag=f"x_raw{a}_1", align_bytes=64)
            t0 = 0
            for grouped in (first, second, third):
                cols = slice(t0, t0 + grouped.shape[1])
                nc.vector.quantize_mx(out=x_words[a][:, cols].bitcast(FP8X4), scales=x_scales[4 * a :, cols], in_=grouped[:].rearrange("p w j -> p (w j)"))
                t0 += grouped.shape[1]
            for g in range(SLOTS // GATHER):
                lists = offs_t[:, g * GATHER // 16 : (g + 1) * GATHER // 16]
                if a == PASSES - 1:
                    nc.vector.tensor_copy(s_scales[g][:], x_scales[:].indirect(lists))
                nc.vector.tensor_copy(s_words[a][g][:], x_words[a][:].indirect(lists))

        for r in range(GATE_EARLY, TOP):
            spread_gate(r)

        for r, pos in enumerate((pos1, pos2, pos3)):
            nc.sync.dma_start(pos_t[r][:], pos)

        codes = {}

        def quantize_w(units, raw_tags, grouped_tag, on_vector):
            total = sum(u[3] for u in units)
            if grouped_tag is None:
                grouped = stage.tile([P, total, PACK], BF16, name="w_grouped", bufs=9, align_bytes=64)
            else:
                grouped = stage.tile([P, total, PACK], BF16, name="w_grouped_held", tag=grouped_tag, bufs=1, align_bytes=64)
            c0 = 0
            for (e, a, n0, width), tag, v in zip(units, raw_tags, on_vector):
                if tag is None:
                    raw = raws.tile([P, PACK, width], F32, name="w_raw", bufs=8)
                else:
                    raw = raws.tile([P, PACK, width], F32, name="w_raw_held", tag=tag, bufs=1)
                rows = w[e, a * K_PASS : (a + 1) * K_PASS, n0 : n0 + width]
                nc.sync.dma_start(out=raw[:], in_=rows.rearrange("(p j) n -> p j n", j=PACK))
                cast(nc.vector.tensor_copy if v else nc.scalar.copy, grouped[:, c0 : c0 + width, :], raw[:])
                c0 += width
            e, a, n0, width = units[0]
            words = held.tile([P, total], U32, name=f"w_words{e}_{a}_{n0}", align_bytes=64)
            scales = held.tile([P, total], U8, name=f"w_scales{e}_{a}_{n0}", align_bytes=64)
            nc.vector.quantize_mx(out=words[:].bitcast(FP8X4), scales=scales[:], in_=grouped[:].rearrange("p w j -> p (w j)"))
            c0 = 0
            for e, a, n0, width in units:
                for h in range(n0 // P, (n0 + width) // P):
                    codes[e, a, h] = (words[:, c0 : c0 + P], scales[:, c0 : c0 + P])
                    c0 += P

        def multiply(h):
            for b in range(SLOTS // BANK):
                acc = psum.tile([P, BANK], F32, name="acc", bufs=3)
                for e in range(b * BANK // C, (b + 1) * BANK // C):
                    g, c0 = divmod(e * C, GATHER)
                    cols = slice(c0, c0 + C)
                    for a in range(PASSES):
                        words, scales = codes[e, a, h]
                        nc.tensor.matmul_mx(out=acc[:, e * C - b * BANK : (e + 1) * C - b * BANK], lhsT=words.bitcast(FP8X4), lhsT_scale=scales,
                                            rhs=s_words[a][g][:, cols].bitcast(FP8X4), rhs_scale=s_scales[g][4 * a :, cols],
                                            start=(a == 0), stop=(a == PASSES - 1))
                nc.scalar.copy(out=y[h][:, b * BANK : (b + 1) * BANK], in_=acc[:])

        def combine(h, holds):
            t0 = 0
            for width in CHUNKS[h]:
                lists = slice(t0 // 16, (t0 + width) // 16)
                prods = []
                for r in range(TOP):
                    if r in holds:
                        picked = stage.tile([P, width], F32, name="picked_held", tag=holds[r], bufs=1, align_bytes=64)
                    else:
                        picked = stage.tile([P, width], F32, name="picked", tag="wide", bufs=7, align_bytes=64)
                    nc.vector.tensor_tensor(picked[:], y[h][:].indirect(pos_t[r][:, lists]), gate_full[r][:, t0 : t0 + width], MULT)
                    prods.append(picked)
                if h == HALVES - 1 and t0 + width == T:
                    part = stage.tile([P, width], F32, name="part")
                    result = stage.tile([P, width], F32, name="result", bufs=3)
                    nc.vector.tensor_tensor(part[:], prods[0][:], prods[1][:], ADD)
                    nc.vector.tensor_tensor(result[:], part[:], prods[2][:], ADD)
                    nc.sync.dma_start(out=out[h * P : (h + 1) * P, t0 : t0 + width], in_=result[:])
                else:
                    for s0 in range(0, width, BANK):
                        span = min(BANK, width - s0)
                        blocks = span // P
                        summed = psum.tile([P, blocks, P], F32, name="summed", tag="turn", bufs=3)
                        for b in range(blocks):
                            for r in range(TOP):
                                nc.tensor.matmul(summed[:, b, :], prods[r][:, s0 + b * P : s0 + (b + 1) * P], ident[:], start=(r == 0), stop=(r == TOP - 1), is_transpose=True)
                        z = stage.tile([P, blocks, P], F32, name="z", bufs=2)
                        nc.scalar.copy(out=z[:], in_=summed[:])
                        back = psum.tile([P, blocks, P], F32, name="back", bufs=2)
                        for b in range(blocks):
                            nc.tensor.transpose(back[:, b, :], z[:, b, :], ident[:])
                        result = stage.tile([P, span], F32, name="result", bufs=3)
                        nc.scalar.copy(out=result[:], in_=back[:].rearrange("p b q -> p (b q)"))
                        nc.sync.dma_start(out=out[h * P : (h + 1) * P, t0 + s0 : t0 + s0 + span], in_=result[:])
                t0 += width

        groups = [[(e, a, 0, N)] for e in range(E - SPLIT) for a in range(PASSES)]
        ends = []
        for h in range(HALVES):
            units = [(e, a, h * P, P) for e in range(E - SPLIT, E) for a in range(PASSES)]
            groups.extend(units[s : s + 2] for s in range(0, len(units), 2))
            ends.append(len(groups) - 1)
        grouped_tags = {ends[1]: "hold_p2", ends[0] + 1: "hold_p1"}
        for late, early in V_GROUPS.items():
            grouped_tags[late] = f"hold_v{late}"
            grouped_tags[early] = f"hold_v{late}"
        raw_tags = {ends[0]: "hold_y0", ends[1]: "hold_y1", 7: "hold_y0", 11: "hold_y1"}
        for i, group in enumerate(groups):
            quantize_w(group, [None] * (len(group) - 1) + [raw_tags.get(i)], grouped_tags.get(i), [i in V_GROUPS] * len(group))
            if i in ends:
                h = ends.index(i)
                y[h] = raws.tile([P, SLOTS + PAD], F32, name="y", tag=f"hold_y{h}", bufs=1)
                nc.gpsimd.memset(y[h][:, SLOTS:], 0.0)
                multiply(h)
        combine(0, {1: "hold_p1", 2: "hold_p2"})
        combine(1, {})
